import numpy as np
import ml_dtypes


def mxq(x, axis, fmt="e4m3"):
    dtype, down = {"e4m3": (ml_dtypes.float8_e4m3fn, 7), "e5m2": (ml_dtypes.float8_e5m2, 14)}[fmt]
    v = np.moveaxis(np.asarray(x, np.float32).astype(ml_dtypes.bfloat16).astype(np.float64), axis, -1)
    blocks = v.reshape(v.shape[:-1] + (-1, 32))
    amax = np.abs(blocks).max(-1, keepdims=True)
    byte = np.maximum(np.where(amax > 0, np.frexp(amax)[1] - 1 + 127, 0) - down, 1)
    scale = np.exp2(byte - 127.0)
    codes = (blocks / scale).astype(np.float32).astype(dtype).astype(np.float64)
    return np.moveaxis((codes * scale).reshape(v.shape), -1, axis)


WIDE = False


def mx_kscale(k):
    if not WIDE:
        return np.ones(k)
    levels = np.array([10, -10, 5, -5, 0])
    if k % 512:
        return np.exp2(np.random.permutation(np.resize(levels, k // 32))).repeat(32)
    a = np.empty((k // 512, 16))
    for p in range(k // 512):
        a[p, :8] = np.random.permutation(np.resize(levels, 8))
        for g in range(8):
            far = levels[np.abs(levels - a[p, g]) >= 10]
            a[p, g + 8] = far[np.random.randint(len(far))]
    return np.exp2(a.ravel()).repeat(32)


def f64(x):
    return np.asarray(x).astype(np.float64)


def striped(idx):
    return np.tile(idx.reshape(-1, 16).T, (8, 1)).astype(np.uint16)


def unstriped(offs):
    return offs[:16].T.reshape(-1).astype(np.int64)


def pack_weight(w):
    k, n = w.shape
    w = f64(np.asarray(w, np.float32).astype(ml_dtypes.bfloat16)).reshape(k // 32, 32, n)
    amax = np.abs(w).max(1)
    byte = np.clip(np.where(amax > 0, np.frexp(amax)[1] - 1 + 127 - 7, 1), 1, 254)
    scaled = (w * np.exp2(127.0 - byte)[:, None, :]).reshape(k, n).astype(np.float32)
    words = np.ascontiguousarray(scaled.reshape(k // 512, 128, 4, n).transpose(0, 1, 3, 2)).astype(ml_dtypes.float8_e4m3fn).view(np.uint8)
    return words, np.ascontiguousarray(byte.astype(np.uint8).reshape(k // 512, 16, n))


def unpack_weight(words, scales):
    g, p, n, _ = words.shape
    vals = np.ascontiguousarray(words).view(ml_dtypes.float8_e4m3fn).astype(np.float64) * np.repeat(np.exp2(scales.astype(np.float64) - 127.0), 8, axis=1)[..., None]
    return vals.transpose(0, 1, 3, 2).reshape(g * 512, n)


K, T, S, V, H, N = 1024, 1024, 512, 256, 512, 128


def setup_inputs():
    n = np.random.standard_normal
    s = mx_kscale(K)[:, None]
    u = mx_kscale(H)
    packed_xT = pack_weight(n((K, T)) * s)
    return {
        "x_words": packed_xT[0],
        "x_scales": packed_xT[1],
        "w1": (n((K, H)) / np.sqrt(K) / s * u).astype(np.float32),
        "w2": (n((H, N)) / np.sqrt(3 * H) / u[:, None]).astype(np.float32),
        "w3": (n((H, N)) / np.sqrt(3 * H) / u[:, None]).astype(np.float32),
        "w4": (n((H, N)) / np.sqrt(3 * H) / u[:, None]).astype(np.float32),
        "offs": striped(np.random.permutation(T)[:S]),
        "pos1": striped(np.random.permutation(S)[:V]),
        "pos2": striped(np.random.permutation(S)[:V]),
        "pos3": striped(np.random.permutation(S)[:V]),
    }


def reference(x_words, x_scales, w1, w2, w3, w4, offs, pos1, pos2, pos3):
    xq = unpack_weight(x_words, x_scales)[:, unstriped(offs)]
    h = mxq(f64(w1), 0, "e4m3").T @ xq
    g0 = h[:, unstriped(pos1)]
    g1 = h[:, unstriped(pos2)]
    g2 = h[:, unstriped(pos3)]
    z1 = (g0 + g1 + g2) / 3
    z2 = np.maximum(np.maximum(g0, g1), g2)
    z3 = np.minimum(np.minimum(g0, g1), g2)
    return mxq(f64(w2), 0, "e4m3").T @ mxq(z1, 0, "e4m3") + mxq(f64(w3), 0, "e4m3").T @ mxq(z2, 0, "e4m3") + mxq(f64(w4), 0, "e4m3").T @ mxq(z3, 0, "e4m3")

@@ -1,0 +1,207 @@
+from contextlib import ExitStack
+
+import concourse.mybir as mybir
+from concourse.masks import make_identity
+
+K, T, S, V, H, N = 1024, 1024, 512, 256, 512, 128
+FLOPS = 2 * K * H * S + 3 * 2 * H * N * V
+
+F32 = mybir.dt.float32
+BF16 = mybir.dt.bfloat16
+I32 = mybir.dt.int32
+U32 = mybir.dt.uint32
+U16 = mybir.dt.uint16
+U8 = mybir.dt.uint8
+FP8X4 = mybir.dt.float8_e4m3fn_x4
+MAX = mybir.AluOpType.max
+MIN = mybir.AluOpType.min
+COPY = mybir.ActivationFunctionType.Copy
+
+P = 128
+PACK = 4
+K_PASS = P * PACK
+PASSES = K // K_PASS
+HALF = H // 2
+D = 3
+
+
+def tile_picked_pna_none_p_kernel(
+    tc, x_words, x_scales, w1, w2, w3, w4, offs, pos1, pos2, pos3, out
+):
+    nc = tc.nc
+    with ExitStack() as ctx:
+        sb = ctx.enter_context(tc.tile_pool(name="sb", bufs=1))
+        ps = ctx.enter_context(tc.psum_pool(name="ps", bufs=1))
+
+        offs_sb = sb.tile([P, S // 16], U16, name="offs_sb")
+        pos_sb = [sb.tile([P, V // 16], U16, name="pos_sb%d" % d) for d in range(D)]
+        x_raw = [sb.tile([P, T], I32, name="x_raw%d" % g) for g in range(PASSES)]
+        xs_raw = sb.tile([P, T], U8, name="xs_raw")
+        w1_raw = [[sb.tile([P, PACK, HALF], F32, name="w1_raw%d%d" % (g, c)) for c in range(2)] for g in range(PASSES)]
+        wo_raw = [sb.tile([P, PACK, N], F32, name="wo_raw%d" % a) for a in range(D)]
+        ident = sb.tile([P, P], F32, name="ident")
+
+        def load_w1(g, c):
+            rows = w1[g * K_PASS : (g + 1) * K_PASS, c * HALF : (c + 1) * HALF]
+            nc.sync.dma_start(out=w1_raw[g][c][:], in_=rows.rearrange("(p j) c -> p j c", j=PACK))
+
+        def load_x(g):
+            nc.sync.dma_start(out=x_raw[g][:], in_=x_words[g].rearrange("p n t -> p (n t)").bitcast(I32))
+
+        nc.vector.memset(xs_raw[:].bitcast(I32), 0)
+        for q in range(4):
+            nc.scalar.dma_start(
+                out=xs_raw[32 * q : 32 * q + 4 * PASSES, :].bitcast(I32),
+                in_=x_scales[:, 4 * q : 4 * q + 4, :].bitcast(I32),
+            )
+        make_identity(nc, ident[:])
+
+        nc.sync.dma_start(out=offs_sb[:], in_=offs)
+        load_w1(0, 0)
+        load_w1(0, 1)
+        load_x(0)
+        load_x(1)
+        load_w1(1, 0)
+        load_w1(1, 1)
+        for d, pos in enumerate((pos1, pos2, pos3)):
+            nc.sync.dma_start(out=pos_sb[d][:], in_=pos)
+        for a, w in enumerate((w2, w3, w4)):
+            nc.sync.dma_start(out=wo_raw[a][:], in_=w.rearrange("(p j) n -> p j n", j=PACK))
+
+        xg = [sb.tile([P, S], U32, name="xg%d" % g, align_bytes=64) for g in range(PASSES)]
+        xsg = sb.tile([P, S], U8, name="xsg", align_bytes=64)
+        w1_bf = [sb.tile([P, PACK, P, PACK], BF16, name="w1_bf%d" % g, align_bytes=64) for g in range(PASSES)]
+        w1_q = [[sb.tile([P, P], U32, name="w1_q%d%d" % (g, t), align_bytes=64) for t in range(PACK)] for g in range(PASSES)]
+        w1_s = [[sb.tile([P, P], U8, name="w1_s%d%d" % (g, t), align_bytes=64) for t in range(PACK)] for g in range(PASSES)]
+        spans = [[(0, S // 2), (S // 2, S)]] + [[(0, S)]] * (PACK - 1)
+        h_ps = [
+            [ps.tile([P, b - a], F32, name="h_ps%d%d" % (t, i), tag="bank%d%d" % (t, i)) for i, (a, b) in enumerate(spans[t])]
+            for t in range(PACK)
+        ]
+        h_sb = [sb.tile([P, S], F32, name="h_sb%d" % t) for t in range(PACK)]
+
+        def cast_w1(copy, g, c):
+            m = HALF // PACK
+            copy(
+                out=w1_bf[g][:, :, c * m : (c + 1) * m, :].rearrange("p t m j -> p m j t"),
+                in_=w1_raw[g][c][:].rearrange("p j (m t) -> p m j t", t=PACK),
+            )
+
+        def gather_x(g):
+            nc.vector.tensor_copy(out=xg[g][:], in_=x_raw[g][:].bitcast(U32).indirect(offs_sb[:]))
+
+        def first_product(g, t):
+            nc.vector.quantize_mx(
+                out=w1_q[g][t][:].bitcast(FP8X4),
+                scales=w1_s[g][t][:],
+                in_=w1_bf[g][:, t, :, :].rearrange("p m j -> p (m j)"),
+            )
+            for i, (a, b) in enumerate(spans[t]):
+                nc.tensor.matmul_mx(
+                    out=h_ps[t][i][:],
+                    lhsT=w1_q[g][t][:].bitcast(FP8X4),
+                    lhsT_scale=w1_s[g][t][:],
+                    rhs=xg[g][:, a:b].bitcast(FP8X4),
+                    rhs_scale=xsg[4 * g : P, a:b],
+                    start=(g == 0),
+                    stop=(g == PASSES - 1),
+                )
+
+        nc.vector.tensor_copy(out=xsg[:], in_=xs_raw[:].indirect(offs_sb[:]))
+        cast_w1(nc.scalar.copy, 0, 0)
+        cast_w1(nc.scalar.copy, 0, 1)
+        gather_x(0)
+        for t in range(PACK):
+            first_product(0, t)
+        gather_x(1)
+        cast_w1(nc.scalar.copy, 1, 0)
+        cast_w1(nc.vector.tensor_copy, 1, 1)
+        for t in range(PACK):
+            first_product(1, t)
+        for t in range(PACK):
+            for i, (a, b) in enumerate(spans[t]):
+                nc.scalar.copy(out=h_sb[t][:, a:b], in_=h_ps[t][i][:])
+
+        wo_bf = [sb.tile([P, N, PACK], BF16, name="wo_bf%d" % a, align_bytes=64) for a in range(D)]
+        wo_q = [sb.tile([P, N], U32, name="wo_q%d" % a, align_bytes=64) for a in range(D)]
+        wo_s = [sb.tile([P, N], U8, name="wo_s%d" % a, align_bytes=64) for a in range(D)]
+        for a in range(D):
+            nc.scalar.copy(
+                out=wo_bf[a][:].rearrange("p (c i) j -> p c j i", i=4),
+                in_=wo_raw[a][:].rearrange("p j (c i) -> p c j i", i=4),
+            )
+
+        g32 = [[sb.tile([P, 2, V], F32, name="g32_%d%d" % (d, u)) for u in range(2)] for d in range(D)]
+        g16 = [sb.tile([P, 2, V, 2], BF16, name="g16_%d" % d) for d in range(D)]
+        sum_ps = [ps.tile([P, 2, 2, P], F32, name="sum_ps%d" % u) for u in range(2)]
+        mean_t = [sb.tile([P, 2, P, 2], BF16, name="mean_t%d" % u) for u in range(2)]
+        back_ps = ps.tile([P, 2, V], F32, name="back_ps")
+        z_bf = [sb.tile([P, V, 2, 2], BF16, name="z_bf%d" % a, align_bytes=64) for a in range(D)]
+        for u in range(2):
+            for e in range(2):
+                for d in range(D):
+                    nc.vector.tensor_copy(out=g32[d][u][:, e, :], in_=h_sb[2 * u + e][:].indirect(pos_sb[d][:]))
+                    for b in range(2):
+                        nc.tensor.matmul(
+                            sum_ps[u][:, b, e, :],
+                            lhsT=g32[d][u][:, e, b * P : (b + 1) * P],
+                            rhs=ident[:],
+                            is_transpose=True,
+                            start=(e == 0 and d == 0 and b == 0),
+                            stop=(e == 1 and d == D - 1 and b == 1),
+                        )
+            for d in range(D):
+                nc.scalar.copy(
+                    out=g16[d][:, u, :, :].rearrange("p (c i) e -> p c e i", i=4),
+                    in_=g32[d][u][:].rearrange("p e (c i) -> p c e i", i=4),
+                )
+            nc.scalar.activation(
+                out=mean_t[u][:], in_=sum_ps[u][:].rearrange("v b e p -> v b p e"), func=COPY, scale=1.0 / D
+            )
+            for b in range(2):
+                nc.tensor.transpose(
+                    back_ps[:, u, b * P : (b + 1) * P],
+                    mean_t[u][:, b, :, :].rearrange("v p e -> v (p e)").bitcast(F32),
+                    ident[:],
+                )
+        nc.scalar.copy(
+            out=z_bf[0][:].rearrange("p v u e -> p (v u e)").bitcast(F32).rearrange("p (v u) -> p v u", u=2),
+            in_=back_ps[:].rearrange("p u v -> p v u"),
+        )
+
+        for a in range(D):
+            nc.vector.quantize_mx(
+                out=wo_q[a][:].bitcast(FP8X4), scales=wo_s[a][:], in_=wo_bf[a][:].rearrange("p n j -> p (n j)")
+            )
+
+        pair = [sb.tile([P, 2, V, 2], BF16, name="pair%d" % a) for a in range(2)]
+        for a, op in enumerate((MAX, MIN)):
+            nc.vector.tensor_tensor(out=pair[a][:], in0=g16[0][:], in1=g16[1][:], op=op)
+        for a, op in enumerate((MAX, MIN)):
+            nc.vector.tensor_tensor(
+                out=z_bf[1 + a][:],
+                in0=pair[a][:].rearrange("p u v e -> p v u e"),
+                in1=g16[2][:].rearrange("p u v e -> p v u e"),
+                op=op,
+            )
+
+        z_q = [sb.tile([P, V], U32, name="z_q%d" % a, align_bytes=64) for a in range(D)]
+        z_s = [sb.tile([P, V], U8, name="z_s%d" % a, align_bytes=64) for a in range(D)]
+        out_ps = ps.tile([P, V], F32, name="out_ps", tag="bank00")
+        order = (1, 2, 0)
+        for a in order:
+            nc.vector.quantize_mx(
+                out=z_q[a][:].bitcast(FP8X4), scales=z_s[a][:], in_=z_bf[a][:].rearrange("p v u e -> p (v u e)")
+            )
+            nc.tensor.matmul_mx(
+                out=out_ps[:],
+                lhsT=wo_q[a][:].bitcast(FP8X4),
+                lhsT_scale=wo_s[a][:],
+                rhs=z_q[a][:].bitcast(FP8X4),
+                rhs_scale=z_s[a][:],
+                start=(a == order[0]),
+                stop=(a == order[-1]),
+            )
+        out_sb = sb.tile([P, V], F32, name="out_sb")
+        nc.vector.tensor_copy(out=out_sb[:], in_=out_ps[:])
+        nc.sync.dma_start(out=out, in_=out_sb[:])

@@ -35,7 +35,7 @@ def tile_picked_pna_none_p_kernel(
 
         offs_sb = sb.tile([P, S // 16], U16, name="offs_sb")
         pos_sb = [sb.tile([P, V // 16], U16, name="pos_sb%d" % d) for d in range(D)]
-        x_raw = [sb.tile([P, T], I32, name="x_raw%d" % g) for g in range(PASSES)]
+        x_raw = [sb.tile([P, T], I32, name="x_raw%d" % g, tag="table%d" % g, align_bytes=64) for g in range(PASSES)]
         xs_raw = sb.tile([P, T], U8, name="xs_raw")
         w1_raw = [[sb.tile([P, PACK, HALF], F32, name="w1_raw%d%d" % (g, c)) for c in range(2)] for g in range(PASSES)]
         wo_raw = [sb.tile([P, PACK, N], F32, name="wo_raw%d" % a) for a in range(D)]
@@ -48,21 +48,25 @@ def tile_picked_pna_none_p_kernel(
         def load_x(g):
             nc.sync.dma_start(out=x_raw[g][:], in_=x_words[g].rearrange("p n t -> p (n t)").bitcast(I32))
 
-        nc.vector.memset(xs_raw[:].bitcast(I32), 0)
-        for q in range(4):
-            nc.scalar.dma_start(
-                out=xs_raw[32 * q : 32 * q + 4 * PASSES, :].bitcast(I32),
-                in_=x_scales[:, 4 * q : 4 * q + 4, :].bitcast(I32),
-            )
+        def load_scales(g):
+            for q in range(4):
+                nc.sync.dma_start(
+                    out=xs_raw[32 * q + 4 * g : 32 * q + 4 * g + 4, :].bitcast(I32),
+                    in_=x_scales[g, 4 * q : 4 * q + 4, :].bitcast(I32),
+                )
+
+        nc.gpsimd.memset(xs_raw[:].bitcast(I32), 0)
         make_identity(nc, ident[:])
 
         nc.sync.dma_start(out=offs_sb[:], in_=offs)
+        load_x(0)
+        load_scales(0)
         load_w1(0, 0)
         load_w1(0, 1)
-        load_x(0)
-        load_x(1)
+        load_scales(1)
         load_w1(1, 0)
         load_w1(1, 1)
+        load_x(1)
         for d, pos in enumerate((pos1, pos2, pos3)):
             nc.sync.dma_start(out=pos_sb[d][:], in_=pos)
         for a, w in enumerate((w2, w3, w4)):
@@ -70,72 +74,92 @@ def tile_picked_pna_none_p_kernel(
 
         xg = [sb.tile([P, S], U32, name="xg%d" % g, align_bytes=64) for g in range(PASSES)]
         xsg = sb.tile([P, S], U8, name="xsg", align_bytes=64)
-        w1_bf = [sb.tile([P, PACK, P, PACK], BF16, name="w1_bf%d" % g, align_bytes=64) for g in range(PASSES)]
-        w1_q = [[sb.tile([P, P], U32, name="w1_q%d%d" % (g, t), align_bytes=64) for t in range(PACK)] for g in range(PASSES)]
-        w1_s = [[sb.tile([P, P], U8, name="w1_s%d%d" % (g, t), align_bytes=64) for t in range(PACK)] for g in range(PASSES)]
-        spans = [[(0, S // 2), (S // 2, S)]] + [[(0, S)]] * (PACK - 1)
+        w1_bf = [sb.tile([P, PACK, P, PACK], BF16, name="w1_bf%d" % g, tag="stage%d" % g, align_bytes=64) for g in range(PASSES)]
+        w1_q = {}
+        w1_s = {}
+        spans = [[(0, S // 2), (S // 2, 3 * S // 4), (3 * S // 4, S)]] + [[(0, S)]] * (PACK - 1)
         h_ps = [
             [ps.tile([P, b - a], F32, name="h_ps%d%d" % (t, i), tag="bank%d%d" % (t, i)) for i, (a, b) in enumerate(spans[t])]
             for t in range(PACK)
         ]
         h_sb = [sb.tile([P, S], F32, name="h_sb%d" % t) for t in range(PACK)]
 
-        def cast_w1(copy, g, c):
-            m = HALF // PACK
+        def cast_w1(copy, g, c, m0=0, m1=HALF // PACK):
+            base = c * HALF // PACK
             copy(
-                out=w1_bf[g][:, :, c * m : (c + 1) * m, :].rearrange("p t m j -> p m j t"),
-                in_=w1_raw[g][c][:].rearrange("p j (m t) -> p m j t", t=PACK),
+                out=w1_bf[g][:, :, base + m0 : base + m1, :].rearrange("p t m j -> p m j t"),
+                in_=w1_raw[g][c][:].rearrange("p j (m t) -> p m j t", t=PACK)[:, m0:m1, :, :],
             )
 
-        def gather_x(g):
-            nc.vector.tensor_copy(out=xg[g][:], in_=x_raw[g][:].bitcast(U32).indirect(offs_sb[:]))
+        def gather_x(g, a, b):
+            nc.vector.tensor_copy(
+                out=xg[g][:, a:b], in_=x_raw[g][:].bitcast(U32).indirect(offs_sb[:, a // 16 : b // 16])
+            )
+
+        def quantize_w1(g, t0, t1, tag):
+            codes = sb.tile([P, (t1 - t0) * P], U32, name="w1_q%d%d" % (g, t0), tag=tag, align_bytes=64)
+            scales = sb.tile([P, (t1 - t0) * P], U8, name="w1_s%d%d" % (g, t0), align_bytes=64)
+            nc.vector.quantize_mx(
+                out=codes[:].bitcast(FP8X4),
+                scales=scales[:],
+                in_=w1_bf[g][:, t0:t1, :, :].rearrange("p t m j -> p (t m j)"),
+            )
+            for t in range(t0, t1):
+                w1_q[g, t] = codes[:, (t - t0) * P : (t - t0 + 1) * P]
+                w1_s[g, t] = scales[:, (t - t0) * P : (t - t0 + 1) * P]
 
         def first_product(g, t):
-            nc.vector.quantize_mx(
-                out=w1_q[g][t][:].bitcast(FP8X4),
-                scales=w1_s[g][t][:],
-                in_=w1_bf[g][:, t, :, :].rearrange("p m j -> p (m j)"),
-            )
             for i, (a, b) in enumerate(spans[t]):
                 nc.tensor.matmul_mx(
                     out=h_ps[t][i][:],
-                    lhsT=w1_q[g][t][:].bitcast(FP8X4),
-                    lhsT_scale=w1_s[g][t][:],
+                    lhsT=w1_q[g, t].bitcast(FP8X4),
+                    lhsT_scale=w1_s[g, t],
                     rhs=xg[g][:, a:b].bitcast(FP8X4),
                     rhs_scale=xsg[4 * g : P, a:b],
                     start=(g == 0),
                     stop=(g == PASSES - 1),
                 )
 
-        nc.vector.tensor_copy(out=xsg[:], in_=xs_raw[:].indirect(offs_sb[:]))
+        gather_x(0, 0, S)
         cast_w1(nc.scalar.copy, 0, 0)
         cast_w1(nc.scalar.copy, 0, 1)
-        gather_x(0)
-        for t in range(PACK):
+        nc.vector.tensor_copy(out=xsg[:], in_=xs_raw[:].indirect(offs_sb[:]))
+        for t in (0, 2):
+            quantize_w1(0, t, t + 2, "codes0%d" % t)
             first_product(0, t)
-        gather_x(1)
+            first_product(0, t + 1)
         cast_w1(nc.scalar.copy, 1, 0)
-        cast_w1(nc.vector.tensor_copy, 1, 1)
-        for t in range(PACK):
-            first_product(1, t)
+        cast_w1(nc.vector.tensor_copy, 1, 1, 0, 40)
+        cast_w1(nc.scalar.copy, 1, 1, 40)
+        quantize_w1(1, 0, 1, "slot10")
+        for a, b in spans[0]:
+            gather_x(1, a, b)
+        first_product(1, 0)
+        quantize_w1(1, 1, 2, "slot11")
+        first_product(1, 1)
+        quantize_w1(1, 2, PACK, "table1")
+        first_product(1, 2)
+        first_product(1, 3)
         for t in range(PACK):
             for i, (a, b) in enumerate(spans[t]):
                 nc.scalar.copy(out=h_sb[t][:, a:b], in_=h_ps[t][i][:])
 
-        wo_bf = [sb.tile([P, N, PACK], BF16, name="wo_bf%d" % a, align_bytes=64) for a in range(D)]
+        wo_tags = ("wo_a", "slot10", "slot11")
+        wo_bf = [sb.tile([P, N, PACK], BF16, name="wo_bf%d" % a, tag=wo_tags[a], align_bytes=64) for a in range(D)]
         wo_q = [sb.tile([P, N], U32, name="wo_q%d" % a, align_bytes=64) for a in range(D)]
         wo_s = [sb.tile([P, N], U8, name="wo_s%d" % a, align_bytes=64) for a in range(D)]
-        for a in range(D):
-            nc.scalar.copy(
+        for a, copy in enumerate((nc.scalar.copy,) * D):
+            copy(
                 out=wo_bf[a][:].rearrange("p (c i) j -> p c j i", i=4),
                 in_=wo_raw[a][:].rearrange("p j (c i) -> p c j i", i=4),
             )
 
         g32 = [[sb.tile([P, 2, V], F32, name="g32_%d%d" % (d, u)) for u in range(2)] for d in range(D)]
         g16 = [sb.tile([P, 2, V, 2], BF16, name="g16_%d" % d) for d in range(D)]
-        sum_ps = [ps.tile([P, 2, 2, P], F32, name="sum_ps%d" % u) for u in range(2)]
-        mean_t = [sb.tile([P, 2, P, 2], BF16, name="mean_t%d" % u) for u in range(2)]
-        back_ps = ps.tile([P, 2, V], F32, name="back_ps")
+        sum_tags = (("sumA", "sumB"), ("bank00", "bank01"))
+        sum_ps = [[ps.tile([P, 2, P], F32, name="sum_ps%d%d" % (u, b), tag=sum_tags[u][b]) for b in range(2)] for u in range(2)]
+        mean_t = [[sb.tile([P, P, 2], BF16, name="mean_t%d%d" % (u, b)) for b in range(2)] for u in range(2)]
+        back_ps = [ps.tile([P, 2, P], F32, name="back_ps%d" % b, tag="bank%d0" % (1 + b)) for b in range(2)]
         z_bf = [sb.tile([P, V, 2, 2], BF16, name="z_bf%d" % a, align_bytes=64) for a in range(D)]
         for u in range(2):
             for e in range(2):
@@ -143,31 +167,28 @@ def tile_picked_pna_none_p_kernel(
                     nc.vector.tensor_copy(out=g32[d][u][:, e, :], in_=h_sb[2 * u + e][:].indirect(pos_sb[d][:]))
                     for b in range(2):
                         nc.tensor.matmul(
-                            sum_ps[u][:, b, e, :],
+                            sum_ps[u][b][:, e, :],
                             lhsT=g32[d][u][:, e, b * P : (b + 1) * P],
                             rhs=ident[:],
                             is_transpose=True,
-                            start=(e == 0 and d == 0 and b == 0),
-                            stop=(e == 1 and d == D - 1 and b == 1),
+                            start=(e == 0 and d == 0),
+                            stop=(e == 1 and d == D - 1),
                         )
             for d in range(D):
                 nc.scalar.copy(
                     out=g16[d][:, u, :, :].rearrange("p (c i) e -> p c e i", i=4),
                     in_=g32[d][u][:].rearrange("p e (c i) -> p c e i", i=4),
                 )
-            nc.scalar.activation(
-                out=mean_t[u][:], in_=sum_ps[u][:].rearrange("v b e p -> v b p e"), func=COPY, scale=1.0 / D
-            )
             for b in range(2):
-                nc.tensor.transpose(
-                    back_ps[:, u, b * P : (b + 1) * P],
-                    mean_t[u][:, b, :, :].rearrange("v p e -> v (p e)").bitcast(F32),
-                    ident[:],
+                nc.scalar.activation(
+                    out=mean_t[u][b][:], in_=sum_ps[u][b][:].rearrange("v e p -> v p e"), func=COPY, scale=1.0 / D
                 )
-        nc.scalar.copy(
-            out=z_bf[0][:].rearrange("p v u e -> p (v u e)").bitcast(F32).rearrange("p (v u) -> p v u", u=2),
-            in_=back_ps[:].rearrange("p u v -> p v u"),
-        )
+                nc.tensor.transpose(
+                    back_ps[b][:, u, :], mean_t[u][b][:].rearrange("v p e -> v (p e)").bitcast(F32), ident[:]
+                )
+        z1_words = z_bf[0][:].rearrange("p v u e -> p (v u e)").bitcast(F32).rearrange("p (v u) -> p v u", u=2)
+        for b in range(2):
+            nc.scalar.copy(out=z1_words[:, b * P : (b + 1) * P, :], in_=back_ps[b][:].rearrange("p u v -> p v u"))
 
         for a in range(D):
             nc.vector.quantize_mx(
@@ -187,21 +208,33 @@ def tile_picked_pna_none_p_kernel(
 
         z_q = [sb.tile([P, V], U32, name="z_q%d" % a, align_bytes=64) for a in range(D)]
         z_s = [sb.tile([P, V], U8, name="z_s%d" % a, align_bytes=64) for a in range(D)]
-        out_ps = ps.tile([P, V], F32, name="out_ps", tag="bank00")
-        order = (1, 2, 0)
-        for a in order:
+        out_ps = [ps.tile([P, P], F32, name="out_ps%d" % b, tag=("bank30", "bank02")[b]) for b in range(2)]
+        out_sb = [sb.tile([P, P], F32, name="out_sb%d" % b) for b in range(2)]
+
+        def quantize_z(a, v0, v1):
             nc.vector.quantize_mx(
-                out=z_q[a][:].bitcast(FP8X4), scales=z_s[a][:], in_=z_bf[a][:].rearrange("p v u e -> p (v u e)")
+                out=z_q[a][:, v0:v1].bitcast(FP8X4),
+                scales=z_s[a][:, v0:v1],
+                in_=z_bf[a][:, v0:v1, :, :].rearrange("p v u e -> p (v u e)"),
             )
+
+        def second_product(a, b, start, stop):
             nc.tensor.matmul_mx(
-                out=out_ps[:],
+                out=out_ps[b][:],
                 lhsT=wo_q[a][:].bitcast(FP8X4),
                 lhsT_scale=wo_s[a][:],
-                rhs=z_q[a][:].bitcast(FP8X4),
-                rhs_scale=z_s[a][:],
-                start=(a == order[0]),
-                stop=(a == order[-1]),
+                rhs=z_q[a][:, b * P : (b + 1) * P].bitcast(FP8X4),
+                rhs_scale=z_s[a][:, b * P : (b + 1) * P],
+                start=start,
+                stop=stop,
             )
-        out_sb = sb.tile([P, V], F32, name="out_sb")
-        nc.vector.tensor_copy(out=out_sb[:], in_=out_ps[:])
-        nc.sync.dma_start(out=out, in_=out_sb[:])
+
+        for a in (1, 2):
+            quantize_z(a, 0, V)
+            for b in range(2):
+                second_product(a, b, a == 1, False)
+        for b, copy in enumerate((nc.scalar.copy, nc.vector.tensor_copy)):
+            quantize_z(0, b * P, (b + 1) * P)
+            second_product(0, b, False, True)
+            copy(out=out_sb[b][:], in_=out_ps[b][:])
+            nc.sync.dma_start(out=out[:, b * P : (b + 1) * P], in_=out_sb[b][:])

from contextlib import ExitStack

import concourse.mybir as mybir
from concourse.masks import make_identity

K, T, S, V, H, N = 1024, 1024, 512, 256, 512, 128
FLOPS = 2 * K * H * S + 3 * 2 * H * N * V

F32 = mybir.dt.float32
BF16 = mybir.dt.bfloat16
I32 = mybir.dt.int32
U32 = mybir.dt.uint32
U16 = mybir.dt.uint16
U8 = mybir.dt.uint8
FP8X4 = mybir.dt.float8_e4m3fn_x4
MAX = mybir.AluOpType.max
MIN = mybir.AluOpType.min
COPY = mybir.ActivationFunctionType.Copy

P = 128
PACK = 4
K_PASS = P * PACK
PASSES = K // K_PASS
HALF = H // 2
D = 3


def tile_picked_pna_none_p_kernel(
    tc, x_words, x_scales, w1, w2, w3, w4, offs, pos1, pos2, pos3, out
):
    nc = tc.nc
    with ExitStack() as ctx:
        sb = ctx.enter_context(tc.tile_pool(name="sb", bufs=1))
        ps = ctx.enter_context(tc.psum_pool(name="ps", bufs=1))

        offs_sb = sb.tile([P, S // 16], U16, name="offs_sb")
        pos_sb = [sb.tile([P, V // 16], U16, name="pos_sb%d" % d) for d in range(D)]
        x_raw = [sb.tile([P, T], I32, name="x_raw%d" % g, tag="table%d" % g, align_bytes=64) for g in range(PASSES)]
        xs_raw = sb.tile([P, T], U8, name="xs_raw")
        w1_raw = [[sb.tile([P, PACK, HALF], F32, name="w1_raw%d%d" % (g, c)) for c in range(2)] for g in range(PASSES)]
        wo_raw = [sb.tile([P, PACK, N], F32, name="wo_raw%d" % a) for a in range(D)]
        ident = sb.tile([P, P], F32, name="ident")

        def load_w1(g, c):
            rows = w1[g * K_PASS : (g + 1) * K_PASS, c * HALF : (c + 1) * HALF]
            nc.sync.dma_start(out=w1_raw[g][c][:], in_=rows.rearrange("(p j) c -> p j c", j=PACK))

        def load_x(g):
            nc.sync.dma_start(out=x_raw[g][:], in_=x_words[g].rearrange("p n t -> p (n t)").bitcast(I32))

        def load_scales(g):
            for q in range(4):
                nc.sync.dma_start(
                    out=xs_raw[32 * q + 4 * g : 32 * q + 4 * g + 4, :].bitcast(I32),
                    in_=x_scales[g, 4 * q : 4 * q + 4, :].bitcast(I32),
                )

        nc.gpsimd.memset(xs_raw[:].bitcast(I32), 0)
        make_identity(nc, ident[:])

        nc.sync.dma_start(out=offs_sb[:], in_=offs)
        load_x(0)
        load_scales(0)
        load_w1(0, 0)
        load_w1(0, 1)
        load_scales(1)
        load_w1(1, 0)
        load_w1(1, 1)
        load_x(1)
        for d, pos in enumerate((pos1, pos2, pos3)):
            nc.sync.dma_start(out=pos_sb[d][:], in_=pos)
        for a, w in enumerate((w2, w3, w4)):
            nc.sync.dma_start(out=wo_raw[a][:], in_=w.rearrange("(p j) n -> p j n", j=PACK))

        xg = [sb.tile([P, S], U32, name="xg%d" % g, align_bytes=64) for g in range(PASSES)]
        xsg = sb.tile([P, S], U8, name="xsg", align_bytes=64)
        w1_bf = [sb.tile([P, PACK, P, PACK], BF16, name="w1_bf%d" % g, tag="stage%d" % g, align_bytes=64) for g in range(PASSES)]
        w1_q = {}
        w1_s = {}
        spans = [[(0, S // 2), (S // 2, 3 * S // 4), (3 * S // 4, S)]] + [[(0, S)]] * (PACK - 1)
        h_ps = [
            [ps.tile([P, b - a], F32, name="h_ps%d%d" % (t, i), tag="bank%d%d" % (t, i)) for i, (a, b) in enumerate(spans[t])]
            for t in range(PACK)
        ]
        h_sb = [sb.tile([P, S], F32, name="h_sb%d" % t) for t in range(PACK)]

        def cast_w1(copy, g, c, m0=0, m1=HALF // PACK):
            base = c * HALF // PACK
            copy(
                out=w1_bf[g][:, :, base + m0 : base + m1, :].rearrange("p t m j -> p m j t"),
                in_=w1_raw[g][c][:].rearrange("p j (m t) -> p m j t", t=PACK)[:, m0:m1, :, :],
            )

        def gather_x(g, a, b):
            nc.vector.tensor_copy(
                out=xg[g][:, a:b], in_=x_raw[g][:].bitcast(U32).indirect(offs_sb[:, a // 16 : b // 16])
            )

        def quantize_w1(g, t0, t1, tag):
            codes = sb.tile([P, (t1 - t0) * P], U32, name="w1_q%d%d" % (g, t0), tag=tag, align_bytes=64)
            scales = sb.tile([P, (t1 - t0) * P], U8, name="w1_s%d%d" % (g, t0), align_bytes=64)
            nc.vector.quantize_mx(
                out=codes[:].bitcast(FP8X4),
                scales=scales[:],
                in_=w1_bf[g][:, t0:t1, :, :].rearrange("p t m j -> p (t m j)"),
            )
            for t in range(t0, t1):
                w1_q[g, t] = codes[:, (t - t0) * P : (t - t0 + 1) * P]
                w1_s[g, t] = scales[:, (t - t0) * P : (t - t0 + 1) * P]

        def first_product(g, t):
            for i, (a, b) in enumerate(spans[t]):
                nc.tensor.matmul_mx(
                    out=h_ps[t][i][:],
                    lhsT=w1_q[g, t].bitcast(FP8X4),
                    lhsT_scale=w1_s[g, t],
                    rhs=xg[g][:, a:b].bitcast(FP8X4),
                    rhs_scale=xsg[4 * g : P, a:b],
                    start=(g == 0),
                    stop=(g == PASSES - 1),
                )

        gather_x(0, 0, S)
        cast_w1(nc.scalar.copy, 0, 0)
        cast_w1(nc.scalar.copy, 0, 1)
        nc.vector.tensor_copy(out=xsg[:], in_=xs_raw[:].indirect(offs_sb[:]))
        for t in (0, 2):
            quantize_w1(0, t, t + 2, "codes0%d" % t)
            first_product(0, t)
            first_product(0, t + 1)
        cast_w1(nc.scalar.copy, 1, 0)
        cast_w1(nc.vector.tensor_copy, 1, 1, 0, 40)
        cast_w1(nc.scalar.copy, 1, 1, 40)
        quantize_w1(1, 0, 1, "slot10")
        for a, b in spans[0]:
            gather_x(1, a, b)
        first_product(1, 0)
        quantize_w1(1, 1, 2, "slot11")
        first_product(1, 1)
        quantize_w1(1, 2, PACK, "table1")
        first_product(1, 2)
        first_product(1, 3)
        for t in range(PACK):
            for i, (a, b) in enumerate(spans[t]):
                nc.scalar.copy(out=h_sb[t][:, a:b], in_=h_ps[t][i][:])

        wo_tags = ("wo_a", "slot10", "slot11")
        wo_bf = [sb.tile([P, N, PACK], BF16, name="wo_bf%d" % a, tag=wo_tags[a], align_bytes=64) for a in range(D)]
        wo_q = [sb.tile([P, N], U32, name="wo_q%d" % a, align_bytes=64) for a in range(D)]
        wo_s = [sb.tile([P, N], U8, name="wo_s%d" % a, align_bytes=64) for a in range(D)]
        for a, copy in enumerate((nc.scalar.copy,) * D):
            copy(
                out=wo_bf[a][:].rearrange("p (c i) j -> p c j i", i=4),
                in_=wo_raw[a][:].rearrange("p j (c i) -> p c j i", i=4),
            )

        g32 = [[sb.tile([P, 2, V], F32, name="g32_%d%d" % (d, u)) for u in range(2)] for d in range(D)]
        g16 = [sb.tile([P, 2, V, 2], BF16, name="g16_%d" % d) for d in range(D)]
        sum_tags = (("sumA", "sumB"), ("bank00", "bank01"))
        sum_ps = [[ps.tile([P, 2, P], F32, name="sum_ps%d%d" % (u, b), tag=sum_tags[u][b]) for b in range(2)] for u in range(2)]
        mean_t = [[sb.tile([P, P, 2], BF16, name="mean_t%d%d" % (u, b)) for b in range(2)] for u in range(2)]
        back_ps = [ps.tile([P, 2, P], F32, name="back_ps%d" % b, tag="bank%d0" % (1 + b)) for b in range(2)]
        z_bf = [sb.tile([P, V, 2, 2], BF16, name="z_bf%d" % a, align_bytes=64) for a in range(D)]
        for u in range(2):
            for e in range(2):
                for d in range(D):
                    nc.vector.tensor_copy(out=g32[d][u][:, e, :], in_=h_sb[2 * u + e][:].indirect(pos_sb[d][:]))
                    for b in range(2):
                        nc.tensor.matmul(
                            sum_ps[u][b][:, e, :],
                            lhsT=g32[d][u][:, e, b * P : (b + 1) * P],
                            rhs=ident[:],
                            is_transpose=True,
                            start=(e == 0 and d == 0),
                            stop=(e == 1 and d == D - 1),
                        )
            for d in range(D):
                nc.scalar.copy(
                    out=g16[d][:, u, :, :].rearrange("p (c i) e -> p c e i", i=4),
                    in_=g32[d][u][:].rearrange("p e (c i) -> p c e i", i=4),
                )
            for b in range(2):
                nc.scalar.activation(
                    out=mean_t[u][b][:], in_=sum_ps[u][b][:].rearrange("v e p -> v p e"), func=COPY, scale=1.0 / D
                )
                nc.tensor.transpose(
                    back_ps[b][:, u, :], mean_t[u][b][:].rearrange("v p e -> v (p e)").bitcast(F32), ident[:]
                )
        z1_words = z_bf[0][:].rearrange("p v u e -> p (v u e)").bitcast(F32).rearrange("p (v u) -> p v u", u=2)
        for b in range(2):
            nc.scalar.copy(out=z1_words[:, b * P : (b + 1) * P, :], in_=back_ps[b][:].rearrange("p u v -> p v u"))

        for a in range(D):
            nc.vector.quantize_mx(
                out=wo_q[a][:].bitcast(FP8X4), scales=wo_s[a][:], in_=wo_bf[a][:].rearrange("p n j -> p (n j)")
            )

        pair = [sb.tile([P, 2, V, 2], BF16, name="pair%d" % a) for a in range(2)]
        for a, op in enumerate((MAX, MIN)):
            nc.vector.tensor_tensor(out=pair[a][:], in0=g16[0][:], in1=g16[1][:], op=op)
        for a, op in enumerate((MAX, MIN)):
            nc.vector.tensor_tensor(
                out=z_bf[1 + a][:],
                in0=pair[a][:].rearrange("p u v e -> p v u e"),
                in1=g16[2][:].rearrange("p u v e -> p v u e"),
                op=op,
            )

        z_q = [sb.tile([P, V], U32, name="z_q%d" % a, align_bytes=64) for a in range(D)]
        z_s = [sb.tile([P, V], U8, name="z_s%d" % a, align_bytes=64) for a in range(D)]
        out_ps = [ps.tile([P, P], F32, name="out_ps%d" % b, tag=("bank30", "bank02")[b]) for b in range(2)]
        out_sb = [sb.tile([P, P], F32, name="out_sb%d" % b) for b in range(2)]

        def quantize_z(a, v0, v1):
            nc.vector.quantize_mx(
                out=z_q[a][:, v0:v1].bitcast(FP8X4),
                scales=z_s[a][:, v0:v1],
                in_=z_bf[a][:, v0:v1, :, :].rearrange("p v u e -> p (v u e)"),
            )

        def second_product(a, b, start, stop):
            nc.tensor.matmul_mx(
                out=out_ps[b][:],
                lhsT=wo_q[a][:].bitcast(FP8X4),
                lhsT_scale=wo_s[a][:],
                rhs=z_q[a][:, b * P : (b + 1) * P].bitcast(FP8X4),
                rhs_scale=z_s[a][:, b * P : (b + 1) * P],
                start=start,
                stop=stop,
            )

        for a in (1, 2):
            quantize_z(a, 0, V)
            for b in range(2):
                second_product(a, b, a == 1, False)
        for b, copy in enumerate((nc.scalar.copy, nc.vector.tensor_copy)):
            quantize_z(0, b * P, (b + 1) * P)
            second_product(0, b, False, True)
            copy(out=out_sb[b][:], in_=out_ps[b][:])
            nc.sync.dma_start(out=out[:, b * P : (b + 1) * P], in_=out_sb[b][:])
